import numpy as np
import ml_dtypes

BF16 = ml_dtypes.bfloat16


def bf(x):
    return np.asarray(x, np.float32).astype(BF16)


def f32(x):
    return np.asarray(x, np.float32)


def f64(x):
    return np.asarray(x).astype(np.float64)


def striped(idx):
    return np.tile(idx.reshape(-1, 16).T, (8, 1))


S, K, M, N, B, Q = 256, 512, 128, 256, 4, 64


def setup_inputs():
    return {"base": bf(np.random.standard_normal((B, M, S))), "x": bf(np.random.standard_normal((K, N))), "w": bf(np.random.standard_normal((K, M)) / np.sqrt(K)), "b": f32(0.5 * np.random.standard_normal((M, 1))), "offs": striped(np.random.permutation(S))}


def reference(base, x, w, b, offs):
    idx = offs[:16].T.reshape(-1)
    z = f64(base).copy()
    for i in range(B):
        z[i][:, idx[i * Q : (i + 1) * Q]] += f64(w).T @ f64(x)[:, i * Q : (i + 1) * Q]
    return z + f64(b)

@@ -1,0 +1,68 @@
+import concourse.mybir as mybir
+from concourse.masks import make_identity
+
+BF16, F32, U16 = mybir.dt.bfloat16, mybir.dt.float32, mybir.dt.uint16
+
+P = 128
+SEQS = 4
+TOKENS = 256
+PIECE = 64
+KBLOCKS = 4
+OFFS_COLS = PIECE // 16
+BANK = 512
+WARMUP = 4
+
+FLOPS = 2 * (KBLOCKS * P) * P * (SEQS * PIECE)
+
+
+def tile_scatter_matmul_kernel(tc, base, x, w, b, offs, out):
+    nc = tc.nc
+    with (
+        tc.tile_pool(name="held", bufs=1) as held,
+        tc.psum_pool(name="banks", bufs=1) as banks,
+    ):
+        offsets = held.tile([P, SEQS * OFFS_COLS], U16, name="offsets")
+        nc.sync.dma_start(offsets[:], offs)
+
+        queues = [nc.sync, nc.scalar]
+        base_sb = [held.tile([P, TOKENS], BF16, name=f"base_sb{i}") for i in range(SEQS)]
+        for i in range(SEQS):
+            queues[i % 2].dma_start(base_sb[i][:], base[i])
+
+        w_sb = held.tile([P, KBLOCKS, P], BF16, name="w_sb")
+        nc.sync.dma_start(w_sb[:], w.rearrange("(p kb) m -> p kb m", kb=KBLOCKS))
+        x_sb = held.tile([P, KBLOCKS, SEQS * PIECE], BF16, name="x_sb")
+        nc.scalar.dma_start(x_sb[:], x.rearrange("(p kb) n -> p kb n", kb=KBLOCKS))
+
+        bias = held.tile([P, 1], F32, name="bias")
+        nc.scalar.dma_start(bias[:], b.rearrange("(a p) o -> p (a o)", p=P))
+
+        zeros = held.tile([P, P], BF16, name="zeros")
+        nc.gpsimd.memset(zeros[:], 0.0)
+        scratch = banks.tile([P, BANK // P, P], F32, name="scratch")
+        for _ in range(WARMUP):
+            nc.tensor.matmul(
+                scratch[:], zeros[:], zeros[:].unsqueeze(1).to_broadcast([P, BANK // P, P]), start=True, stop=True
+            )
+
+        ident = held.tile([P, P], BF16, name="ident")
+        make_identity(nc, ident[:])
+
+        windows = [banks.tile([P, TOKENS], F32, name=f"window{i}") for i in range(SEQS)]
+        for i in range(SEQS):
+            nc.tensor.matmul(windows[i][:], ident[:], base_sb[i][:], start=True, stop=False)
+
+        for i in range(SEQS):
+            piece = offsets[:, i * OFFS_COLS : (i + 1) * OFFS_COLS]
+            for kb in range(KBLOCKS):
+                nc.tensor.matmul(
+                    windows[i][:].indirect(piece),
+                    w_sb[:, kb, :],
+                    x_sb[:, kb, i * PIECE : (i + 1) * PIECE],
+                    start=False,
+                    stop=(kb == KBLOCKS - 1),
+                )
+
+            z = held.tile([P, TOKENS], F32, name=f"z{i}")
+            nc.vector.tensor_scalar_add(z[:], windows[i][:], bias[:, 0:1])
+            queues[i % 2].dma_start(out[i], z[:])

@@ -21,13 +21,13 @@ def tile_scatter_matmul_kernel(tc, base, x, w, b, offs, out):
         tc.tile_pool(name="held", bufs=1) as held,
         tc.psum_pool(name="banks", bufs=1) as banks,
     ):
-        offsets = held.tile([P, SEQS * OFFS_COLS], U16, name="offsets")
-        nc.sync.dma_start(offsets[:], offs)
-
         queues = [nc.sync, nc.scalar]
         base_sb = [held.tile([P, TOKENS], BF16, name=f"base_sb{i}") for i in range(SEQS)]
         for i in range(SEQS):
             queues[i % 2].dma_start(base_sb[i][:], base[i])
+
+        offsets = held.tile([P, SEQS * OFFS_COLS], U16, name="offsets")
+        nc.sync.dma_start(offsets[:], offs)
 
         w_sb = held.tile([P, KBLOCKS, P], BF16, name="w_sb")
         nc.sync.dma_start(w_sb[:], w.rearrange("(p kb) m -> p kb m", kb=KBLOCKS))

@@ -10,6 +10,7 @@ PIECE = 64
 KBLOCKS = 4
 OFFS_COLS = PIECE // 16
 BANK = 512
+ALIGN = 256
 WARMUP = 4
 
 FLOPS = 2 * (KBLOCKS * P) * P * (SEQS * PIECE)
@@ -22,16 +23,16 @@ def tile_scatter_matmul_kernel(tc, base, x, w, b, offs, out):
         tc.psum_pool(name="banks", bufs=1) as banks,
     ):
         queues = [nc.sync, nc.scalar]
-        base_sb = [held.tile([P, TOKENS], BF16, name=f"base_sb{i}") for i in range(SEQS)]
+        base_sb = [held.tile([P, TOKENS], BF16, name=f"base_sb{i}", align_bytes=ALIGN) for i in range(SEQS)]
         for i in range(SEQS):
             queues[i % 2].dma_start(base_sb[i][:], base[i])
 
         offsets = held.tile([P, SEQS * OFFS_COLS], U16, name="offsets")
         nc.sync.dma_start(offsets[:], offs)
 
-        w_sb = held.tile([P, KBLOCKS, P], BF16, name="w_sb")
+        w_sb = held.tile([P, KBLOCKS, P], BF16, name="w_sb", align_bytes=ALIGN)
         nc.sync.dma_start(w_sb[:], w.rearrange("(p kb) m -> p kb m", kb=KBLOCKS))
-        x_sb = held.tile([P, KBLOCKS, SEQS * PIECE], BF16, name="x_sb")
+        x_sb = held.tile([P, KBLOCKS, SEQS * PIECE], BF16, name="x_sb", align_bytes=ALIGN)
         nc.scalar.dma_start(x_sb[:], x.rearrange("(p kb) n -> p kb n", kb=KBLOCKS))
 
         bias = held.tile([P, 1], F32, name="bias")
@@ -63,6 +64,6 @@ def tile_scatter_matmul_kernel(tc, base, x, w, b, offs, out):
                     stop=(kb == KBLOCKS - 1),
                 )
 
-            z = held.tile([P, TOKENS], F32, name=f"z{i}")
+            z = held.tile([P, TOKENS], F32, name=f"z{i}", align_bytes=ALIGN)
             nc.vector.tensor_scalar_add(z[:], windows[i][:], bias[:, 0:1])
             queues[i % 2].dma_start(out[i], z[:])

@@ -5,9 +5,12 @@ BF16, F32, U16 = mybir.dt.bfloat16, mybir.dt.float32, mybir.dt.uint16
 
 P = 128
 SEQS = 4
+PAIR = 2
 TOKENS = 256
 PIECE = 64
 KBLOCKS = 4
+HALF = 2
+BLOCK = 32
 OFFS_COLS = PIECE // 16
 BANK = 512
 ALIGN = 256
@@ -22,21 +25,31 @@ def tile_scatter_matmul_kernel(tc, base, x, w, b, offs, out):
         tc.tile_pool(name="held", bufs=1) as held,
         tc.psum_pool(name="banks", bufs=1) as banks,
     ):
+        base_sb = [
+            held.tile([P, PAIR, TOKENS], BF16, name=f"base_sb{h}", align_bytes=ALIGN) for h in range(SEQS // PAIR)
+        ]
         queues = [nc.sync, nc.scalar]
-        base_sb = [held.tile([P, TOKENS], BF16, name=f"base_sb{i}", align_bytes=ALIGN) for i in range(SEQS)]
-        for i in range(SEQS):
-            queues[i % 2].dma_start(base_sb[i][:], base[i])
+        for h in range(SEQS // PAIR):
+            queues[h].dma_start(base_sb[h][:], base[h * PAIR : (h + 1) * PAIR].rearrange("i m t -> m i t"))
 
         offsets = held.tile([P, SEQS * OFFS_COLS], U16, name="offsets")
         nc.sync.dma_start(offsets[:], offs)
 
         w_sb = held.tile([P, KBLOCKS, P], BF16, name="w_sb", align_bytes=ALIGN)
         nc.sync.dma_start(w_sb[:], w.rearrange("(p kb) m -> p kb m", kb=KBLOCKS))
-        x_sb = held.tile([P, KBLOCKS, SEQS * PIECE], BF16, name="x_sb", align_bytes=ALIGN)
-        nc.scalar.dma_start(x_sb[:], x.rearrange("(p kb) n -> p kb n", kb=KBLOCKS))
+        x_cut = x.rearrange("(p kb) n -> p kb n", kb=KBLOCKS)
+        x_sb = [
+            held.tile([P, HALF, SEQS * PIECE], BF16, name=f"x_sb{h}", align_bytes=ALIGN) for h in range(KBLOCKS // HALF)
+        ]
+        nc.scalar.dma_start(x_sb[0][:], x_cut[:, 0:HALF, :])
 
-        bias = held.tile([P, 1], F32, name="bias")
-        nc.scalar.dma_start(bias[:], b.rearrange("(a p) o -> p (a o)", p=P))
+        b_rows = held.tile([P, BLOCK], F32, name="b_rows", align_bytes=ALIGN)
+        nc.vector.memset(b_rows[:], 0.0)
+        nc.scalar.dma_start(b_rows[0:P:BLOCK, :], b.rearrange("(g c) o -> g (c o)", c=BLOCK))
+        bias = held.tile([P, BLOCK], F32, name="bias", align_bytes=ALIGN)
+        nc.vector.transpose(bias[:], b_rows[:])
+
+        nc.sync.dma_start(x_sb[1][:], x_cut[:, HALF:KBLOCKS, :])
 
         zeros = held.tile([P, P], BF16, name="zeros")
         nc.gpsimd.memset(zeros[:], 0.0)
@@ -51,18 +64,25 @@ def tile_scatter_matmul_kernel(tc, base, x, w, b, offs, out):
 
         windows = [banks.tile([P, TOKENS], F32, name=f"window{i}") for i in range(SEQS)]
         for i in range(SEQS):
-            nc.tensor.matmul(windows[i][:], ident[:], base_sb[i][:], start=True, stop=False)
+            nc.tensor.matmul(windows[i][:], ident[:], base_sb[i // PAIR][:, i % PAIR, :], start=True, stop=False)
 
-        for i in range(SEQS):
+        def scatter(i, half):
             piece = offsets[:, i * OFFS_COLS : (i + 1) * OFFS_COLS]
-            for kb in range(KBLOCKS):
+            for kb in range(half * HALF, (half + 1) * HALF):
                 nc.tensor.matmul(
                     windows[i][:].indirect(piece),
                     w_sb[:, kb, :],
-                    x_sb[:, kb, i * PIECE : (i + 1) * PIECE],
+                    x_sb[half][:, kb % HALF, i * PIECE : (i + 1) * PIECE],
                     start=False,
                     stop=(kb == KBLOCKS - 1),
                 )
+
+        for i in range(PAIR):
+            scatter(i, 0)
+        for i in range(SEQS):
+            if i >= PAIR:
+                scatter(i, 0)
+            scatter(i, 1)
 
             z = held.tile([P, TOKENS], F32, name=f"z{i}", align_bytes=ALIGN)
             nc.vector.tensor_scalar_add(z[:], windows[i][:], bias[:, 0:1])

@@ -14,7 +14,7 @@ BLOCK = 32
 OFFS_COLS = PIECE // 16
 BANK = 512
 ALIGN = 256
-WARMUP = 4
+WARMUP = 5
 
 FLOPS = 2 * (KBLOCKS * P) * P * (SEQS * PIECE)
 
@@ -32,7 +32,7 @@ def tile_scatter_matmul_kernel(tc, base, x, w, b, offs, out):
         for h in range(SEQS // PAIR):
             queues[h].dma_start(base_sb[h][:], base[h * PAIR : (h + 1) * PAIR].rearrange("i m t -> m i t"))
 
-        offsets = held.tile([P, SEQS * OFFS_COLS], U16, name="offsets")
+        offsets = held.tile([P, SEQS * OFFS_COLS], U16, name="offsets", align_bytes=ALIGN)
         nc.sync.dma_start(offsets[:], offs)
 
         w_sb = held.tile([P, KBLOCKS, P], BF16, name="w_sb", align_bytes=ALIGN)

@@ -14,7 +14,7 @@ BLOCK = 32
 OFFS_COLS = PIECE // 16
 BANK = 512
 ALIGN = 256
-WARMUP = 5
+WARMUP = 3
 
 FLOPS = 2 * (KBLOCKS * P) * P * (SEQS * PIECE)
 

import concourse.mybir as mybir
from concourse.masks import make_identity

BF16, F32, U16 = mybir.dt.bfloat16, mybir.dt.float32, mybir.dt.uint16

P = 128
SEQS = 4
PAIR = 2
TOKENS = 256
PIECE = 64
KBLOCKS = 4
HALF = 2
BLOCK = 32
OFFS_COLS = PIECE // 16
BANK = 512
ALIGN = 256
WARMUP = 3

FLOPS = 2 * (KBLOCKS * P) * P * (SEQS * PIECE)


def tile_scatter_matmul_kernel(tc, base, x, w, b, offs, out):
    nc = tc.nc
    with (
        tc.tile_pool(name="held", bufs=1) as held,
        tc.psum_pool(name="banks", bufs=1) as banks,
    ):
        base_sb = [
            held.tile([P, PAIR, TOKENS], BF16, name=f"base_sb{h}", align_bytes=ALIGN) for h in range(SEQS // PAIR)
        ]
        queues = [nc.sync, nc.scalar]
        for h in range(SEQS // PAIR):
            queues[h].dma_start(base_sb[h][:], base[h * PAIR : (h + 1) * PAIR].rearrange("i m t -> m i t"))

        offsets = held.tile([P, SEQS * OFFS_COLS], U16, name="offsets", align_bytes=ALIGN)
        nc.sync.dma_start(offsets[:], offs)

        w_sb = held.tile([P, KBLOCKS, P], BF16, name="w_sb", align_bytes=ALIGN)
        nc.sync.dma_start(w_sb[:], w.rearrange("(p kb) m -> p kb m", kb=KBLOCKS))
        x_cut = x.rearrange("(p kb) n -> p kb n", kb=KBLOCKS)
        x_sb = [
            held.tile([P, HALF, SEQS * PIECE], BF16, name=f"x_sb{h}", align_bytes=ALIGN) for h in range(KBLOCKS // HALF)
        ]
        nc.scalar.dma_start(x_sb[0][:], x_cut[:, 0:HALF, :])

        b_rows = held.tile([P, BLOCK], F32, name="b_rows", align_bytes=ALIGN)
        nc.vector.memset(b_rows[:], 0.0)
        nc.scalar.dma_start(b_rows[0:P:BLOCK, :], b.rearrange("(g c) o -> g (c o)", c=BLOCK))
        bias = held.tile([P, BLOCK], F32, name="bias", align_bytes=ALIGN)
        nc.vector.transpose(bias[:], b_rows[:])

        nc.sync.dma_start(x_sb[1][:], x_cut[:, HALF:KBLOCKS, :])

        zeros = held.tile([P, P], BF16, name="zeros")
        nc.gpsimd.memset(zeros[:], 0.0)
        scratch = banks.tile([P, BANK // P, P], F32, name="scratch")
        for _ in range(WARMUP):
            nc.tensor.matmul(
                scratch[:], zeros[:], zeros[:].unsqueeze(1).to_broadcast([P, BANK // P, P]), start=True, stop=True
            )

        ident = held.tile([P, P], BF16, name="ident")
        make_identity(nc, ident[:])

        windows = [banks.tile([P, TOKENS], F32, name=f"window{i}") for i in range(SEQS)]
        for i in range(SEQS):
            nc.tensor.matmul(windows[i][:], ident[:], base_sb[i // PAIR][:, i % PAIR, :], start=True, stop=False)

        def scatter(i, half):
            piece = offsets[:, i * OFFS_COLS : (i + 1) * OFFS_COLS]
            for kb in range(half * HALF, (half + 1) * HALF):
                nc.tensor.matmul(
                    windows[i][:].indirect(piece),
                    w_sb[:, kb, :],
                    x_sb[half][:, kb % HALF, i * PIECE : (i + 1) * PIECE],
                    start=False,
                    stop=(kb == KBLOCKS - 1),
                )

        for i in range(PAIR):
            scatter(i, 0)
        for i in range(SEQS):
            if i >= PAIR:
                scatter(i, 0)
            scatter(i, 1)

            z = held.tile([P, TOKENS], F32, name=f"z{i}", align_bytes=ALIGN)
            nc.vector.tensor_scalar_add(z[:], windows[i][:], bias[:, 0:1])
            queues[i % 2].dma_start(out[i], z[:])
